import numpy as np
import ml_dtypes


def mxq(x, axis, fmt="e4m3"):
    dtype, down = {"e4m3": (ml_dtypes.float8_e4m3fn, 7), "e5m2": (ml_dtypes.float8_e5m2, 14)}[fmt]
    v = np.moveaxis(np.asarray(x, np.float32).astype(ml_dtypes.bfloat16).astype(np.float64), axis, -1)
    blocks = v.reshape(v.shape[:-1] + (-1, 32))
    amax = np.abs(blocks).max(-1, keepdims=True)
    byte = np.maximum(np.where(amax > 0, np.frexp(amax)[1] - 1 + 127, 0) - down, 1)
    scale = np.exp2(byte - 127.0)
    codes = (blocks / scale).astype(np.float32).astype(dtype).astype(np.float64)
    return np.moveaxis((codes * scale).reshape(v.shape), -1, axis)


WIDE = False


def mx_kscale(k):
    if not WIDE:
        return np.ones(k)
    levels = np.array([10, -10, 5, -5, 0])
    if k % 512:
        return np.exp2(np.random.permutation(np.resize(levels, k // 32))).repeat(32)
    a = np.empty((k // 512, 16))
    for p in range(k // 512):
        a[p, :8] = np.random.permutation(np.resize(levels, 8))
        for g in range(8):
            far = levels[np.abs(levels - a[p, g]) >= 10]
            a[p, g + 8] = far[np.random.randint(len(far))]
    return np.exp2(a.ravel()).repeat(32)


def f64(x):
    return np.asarray(x).astype(np.float64)


def striped(idx):
    return np.tile(idx.reshape(-1, 16).T, (8, 1)).astype(np.uint16)


def unstriped(offs):
    return offs[:16].T.reshape(-1).astype(np.int64)


def relu(v):
    return np.maximum(v, 0.0)


K, T, E, C, N = 512, 512, 16, 128, 512
TOP = 4
M = 512


def by_expert(wq, xq):
    return np.concatenate([wq[e].T @ xq[:, e * C:(e + 1) * C] for e in range(E)], axis=1)


def setup_inputs():
    n = np.random.standard_normal
    s = mx_kscale(K)[:, None]
    v = mx_kscale(N)
    deal = np.repeat(np.arange(E), C).reshape(TOP, T)[:, np.random.permutation(T)]
    deal = np.take_along_axis(deal, np.argsort(np.random.rand(TOP, T), axis=0), axis=0)
    for _ in range(8):
        s_, t_ = np.random.permutation(T).reshape(2, -1); r = np.random.randint(TOP, size=T // 2); x, y = deal[r, s_].copy(), deal[r, t_].copy()
        ok = ~((deal[:, s_] == y).any(0) | (deal[:, t_] == x).any(0)); deal[r[ok], s_[ok]] = y[ok]; deal[r[ok], t_[ok]] = x[ok]
    order = np.lexsort((np.random.rand(TOP * T), deal.reshape(-1)))
    slot_token = order % T; pos = np.empty(TOP * T, np.int64); pos[order] = np.arange(TOP * T); pos = pos.reshape(TOP, T)
    g = np.random.uniform(0.5, 1.5, (TOP, T)); g = g / g.sum(0)
    return {
        "xT": (n((K, T)) * s).astype(np.float32),
        "w": (n((E, K, N)) / np.sqrt(K) / s[None] * v[None, None, :]).astype(np.float32),
        "b": (0.3 * n((N, E)) * v[:, None]).astype(np.float32),
        "wp": (n((N, M)) / np.sqrt(N) / v[:, None]).astype(np.float32),
        "gate": np.stack([np.tile(r, (N, 1)) for r in g]).astype(np.float32),
        "offs": striped(slot_token),
        "pos1": striped(pos[0]),
        "pos2": striped(pos[1]),
        "pos3": striped(pos[2]),
        "pos4": striped(pos[3]),
    }


def reference(xT, w, b, wp, gate, offs, pos1, pos2, pos3, pos4):
    idx = unstriped(offs)
    xq = mxq(f64(xT)[:, idx], 0, "e4m3")
    y = by_expert(mxq(f64(w), 1, "e4m3"), xq)
    y = relu(y + np.repeat(f64(b), C, axis=1))
    c = f64(gate[0]) * y[:, unstriped(pos1)] + f64(gate[1]) * y[:, unstriped(pos2)] + f64(gate[2]) * y[:, unstriped(pos3)] + f64(gate[3]) * y[:, unstriped(pos4)]
    return mxq(f64(wp), 0, "e4m3").T @ mxq(c, 0, "e4m3")

@@ -1,0 +1,238 @@
+from contextlib import ExitStack
+
+import concourse.mybir as mybir
+from concourse.masks import make_identity
+
+K, T, E, C, N, M, TOP = 512, 512, 16, 128, 512, 512, 4
+S = E * C
+P = 128
+PACK = 4
+FLOPS = 2 * K * N * S + 2 * N * M * T
+BYTES = 4 * (K * T + E * K * N + N * E + N * M + TOP * P * T + M * T) + 2 * P * (S + TOP * T) // 16
+
+F32 = mybir.dt.float32
+BF16 = mybir.dt.bfloat16
+U32 = mybir.dt.uint32
+U16 = mybir.dt.uint16
+U8 = mybir.dt.uint8
+FP8X4 = mybir.dt.float8_e4m3fn_x4
+RELU = mybir.ActivationFunctionType.Relu
+MULT = mybir.AluOpType.mult
+
+UNITS = [[(4 * g + q, j, 1) for q in range(4)] for j in range(4) for g in range(4)]
+VECTOR_COLS = [0] * 4 + [208] * 12
+GATHER = 256
+PIECES = [256, 128, 128]
+GATE_AFTER = 2
+WP_AFTER = 13
+COMBINE_LAG = 2
+
+
+def interleave(copy, grouped, raw, c0, c1):
+    copy(
+        grouped[:, c0:c1, :].rearrange("p (c i) t -> p c t i", i=2),
+        raw[:, :, c0:c1].rearrange("p t (c i) -> p c t i", i=2),
+    )
+
+
+def tile_moe_nxt_lin_relu_kernel(
+    tc, xT, w, b, wp, gate, offs, pos1, pos2, pos3, pos4, out
+):
+    nc = tc.nc
+    with ExitStack() as ctx:
+        keep = ctx.enter_context(tc.tile_pool(name="keep", bufs=1))
+        raws = ctx.enter_context(tc.tile_pool(name="raws", bufs=10))
+        work = ctx.enter_context(tc.tile_pool(name="work", bufs=4))
+        prods = ctx.enter_context(tc.tile_pool(name="prods", bufs=8))
+        psum = ctx.enter_context(tc.psum_pool(name="psum", bufs=8))
+
+        def bank():
+            return psum.tile([P, 512], F32, name="bank")
+
+        x_raw = keep.tile([P, PACK, T], F32, name="x_raw")
+        x_rows = xT.rearrange("(p j) t -> p j t", j=PACK)
+        for h in range(2):
+            nc.sync.dma_start(out=x_raw[:, :, h * 256:(h + 1) * 256], in_=x_rows[:, :, h * 256:(h + 1) * 256])
+        offs_sb = keep.tile([P, S // 16], U16, name="offs_sb")
+        nc.sync.dma_start(offs_sb[:], offs)
+        x_words = keep.tile([P, T], U32, name="x_words", align_bytes=64)
+        x_bytes = keep.tile([P, T], U8, name="x_bytes", align_bytes=64)
+        nc.gpsimd.memset(x_bytes[:], 0)
+        ident = keep.tile([P, P], F32, name="ident")
+        make_identity(nc, ident[:])
+        x_bf = keep.tile([P, T, PACK], BF16, name="x_bf", align_bytes=64)
+        interleave(nc.vector.tensor_copy, x_bf, x_raw, 0, 256)
+        interleave(nc.scalar.copy, x_bf, x_raw, 256, 384)
+        interleave(nc.vector.tensor_copy, x_bf, x_raw, 384, 512)
+        for h in range(2):
+            nc.vector.quantize_mx(
+                out=x_words[:, h * 256:(h + 1) * 256].bitcast(FP8X4),
+                scales=x_bytes[:, h * 256:(h + 1) * 256],
+                in_=x_bf[:, h * 256:(h + 1) * 256, :].rearrange("p c t -> p (c t)"),
+            )
+        slot_words = keep.tile([P, S], U32, name="slot_words", align_bytes=64)
+        slot_bytes = keep.tile([P, S], U8, name="slot_bytes", align_bytes=64)
+        gathered = set()
+
+        def gather_slots(e):
+            g = e * C // GATHER
+            if g in gathered:
+                return
+            gathered.add(g)
+            cols = slice(g * GATHER, (g + 1) * GATHER)
+            entries = offs_sb[:, g * GATHER // 16:(g + 1) * GATHER // 16]
+            nc.vector.tensor_copy(slot_words[:, cols], x_words[:].indirect(entries))
+            nc.vector.tensor_copy(slot_bytes[:, cols], x_bytes[:].indirect(entries))
+
+        bias = keep.tile([P, PACK, E], F32, name="bias")
+        y = [keep.tile([P, S], F32, name="y%d" % j) for j in range(4)]
+        gate_sb = keep.tile([P, TOP, T], F32, name="gate_sb")
+        pos_sb = [keep.tile([P, T // 16], U16, name="pos%d" % i) for i in range(TOP)]
+        cT = keep.tile([P, 4, 2, P, 2], BF16, name="cT")
+        wp_words = keep.tile([P, M], U32, name="wp_words", align_bytes=64)
+        wp_bytes = keep.tile([P, M], U8, name="wp_bytes", align_bytes=64)
+
+        def quantise(raw, vcols, words, scales):
+            grouped = work.tile([P, 512, PACK], BF16, name="grouped", align_bytes=64)
+            if vcols > 0:
+                interleave(nc.vector.tensor_copy, grouped, raw, 0, vcols)
+            if vcols < 512:
+                interleave(nc.scalar.copy, grouped, raw, vcols, 512)
+            nc.vector.quantize_mx(
+                out=words[:].bitcast(FP8X4), scales=scales[:], in_=grouped[:].rearrange("p c t -> p (c t)")
+            )
+
+        def run_unit(u):
+            raw = raws.tile([P, PACK, 512], F32, name="raw")
+            col = 0
+            for e, j0, nj in UNITS[u]:
+                nc.sync.dma_start(
+                    out=raw[:, :, col:col + nj * P],
+                    in_=w[e].rearrange("(p j) n -> p j n", j=PACK)[:, :, j0 * P:(j0 + nj) * P],
+                )
+                col += nj * P
+            if u == 0:
+                nc.sync.dma_start(out=bias[:], in_=b.rearrange("(j p) e -> p j e", p=P))
+            for e, j0, nj in UNITS[u]:
+                gather_slots(e)
+            words = work.tile([P, 512], U32, name="words", align_bytes=64)
+            scales = work.tile([P, 512], U8, name="scales", align_bytes=64)
+            quantise(raw, VECTOR_COLS[u], words, scales)
+            acc = bank()
+            parts = [(e, j) for e, j0, nj in UNITS[u] for j in range(j0, j0 + nj)]
+            for q, (e, j) in enumerate(parts):
+                cols = slice(q * P, (q + 1) * P)
+                slots = slice(e * C, (e + 1) * C)
+                nc.tensor.matmul_mx(
+                    out=acc[:, cols],
+                    lhsT=words[:, cols].bitcast(FP8X4), lhsT_scale=scales[:, cols],
+                    rhs=slot_words[:, slots].bitcast(FP8X4), rhs_scale=slot_bytes[:, slots],
+                    start=True, stop=True,
+                )
+            for q, (e, j) in enumerate(parts):
+                nc.scalar.activation(
+                    y[j][:, e * C:(e + 1) * C], acc[:, q * P:(q + 1) * P], RELU, bias=bias[:, j, e:e + 1]
+                )
+            return parts
+
+        def products(j, t0, nt):
+            made = []
+            for i in range(TOP):
+                prod = prods.tile([P, T], F32, name="prod")
+                nc.vector.tensor_tensor(
+                    prod[:, 0:nt],
+                    y[j][:].indirect(pos_sb[i][:, t0 // 16:(t0 + nt) // 16]),
+                    gate_sb[:, i, t0:t0 + nt],
+                    MULT,
+                )
+                made.append(prod)
+            return made
+
+        def round_sums(copy, acc, j, blk0, nblk):
+            copy(
+                cT[:, blk0:blk0 + nblk, :, 32 * j:32 * (j + 1), :].rearrange("t b u p e -> t u b p e"),
+                acc[:, 0:nblk * P].rearrange("t (b p u e) -> t u b p e", b=nblk, u=2, e=2),
+            )
+
+        def combine(j):
+            made = products(j, 0, T)
+            acc = bank()
+            for blk in range(4):
+                cols = slice(blk * P, (blk + 1) * P)
+                for i in range(TOP):
+                    nc.tensor.matmul(acc[:, cols], made[i][:, cols], ident[:], start=(i == 0), stop=(i == TOP - 1), is_transpose=True)
+            round_sums(nc.scalar.copy, acc, j, 0, 4)
+
+        def finish(j, t0, nt, last):
+            made = products(j, t0, nt)
+            nblk = nt // P
+            accs = [bank() for blk in range(nblk)]
+            for i in range(TOP):
+                for blk in range(nblk):
+                    nc.tensor.matmul(accs[blk][:, 0:P], made[i][:, blk * P:(blk + 1) * P], ident[:], start=(i == 0), stop=(i == TOP - 1), is_transpose=True)
+            c_bf = work.tile([P, 256, PACK], BF16, name="c_bf", align_bytes=64)
+            for blk in range(nblk):
+                tb = t0 // P + blk
+                round_sums(nc.scalar.copy, accs[blk], j, tb, 1)
+                turned = bank()
+                for u in range(2):
+                    nc.tensor.transpose(
+                        turned[:, u * P:(u + 1) * P],
+                        cT[:, tb, u, :, :].rearrange("t p e -> t (p e)").bitcast(F32),
+                        ident[:],
+                    )
+                nc.scalar.copy(
+                    c_bf[:, blk * P:(blk + 1) * P, :].rearrange("p t k -> p (t k)").bitcast(F32).rearrange("p (t u) -> p t u", u=2),
+                    turned[:, 0:2 * P].rearrange("p (u t) -> p t u", u=2),
+                )
+            c_words = work.tile([P, 256], U32, name="c_words", align_bytes=64)
+            c_bytes = work.tile([P, 256], U8, name="c_bytes", align_bytes=64)
+            nc.vector.quantize_mx(
+                out=c_words[:, 0:nt].bitcast(FP8X4), scales=c_bytes[:, 0:nt],
+                in_=c_bf[:, 0:nt, :].rearrange("p t k -> p (t k)"),
+            )
+            for half in range(2):
+                res = bank()
+                for q in range(2):
+                    f = slice((2 * half + q) * P, (2 * half + q + 1) * P)
+                    nc.tensor.matmul_mx(
+                        out=res[:, q * nt:(q + 1) * nt],
+                        lhsT=wp_words[:, f].bitcast(FP8X4), lhsT_scale=wp_bytes[:, f],
+                        rhs=c_words[:, 0:nt].bitcast(FP8X4), rhs_scale=c_bytes[:, 0:nt],
+                        start=True, stop=True,
+                    )
+                staged = work.tile([P, 512], F32, name="staged")
+                if last and half == 1:
+                    nc.vector.tensor_copy(staged[:, 0:2 * nt], res[:, 0:2 * nt])
+                else:
+                    nc.scalar.copy(staged[:, 0:2 * nt], res[:, 0:2 * nt])
+                nc.sync.dma_start(
+                    out=out[half * 256:(half + 1) * 256, t0:t0 + nt].rearrange("(q p) t -> p q t", p=P),
+                    in_=staged[:, 0:2 * nt].rearrange("p (q t) -> p q t", q=2),
+                )
+
+        done = [0, 0, 0, 0]
+        due = []
+        for u in range(len(UNITS)):
+            for e, j in run_unit(u):
+                done[j] += 1
+                if done[j] == E:
+                    due.append((u + COMBINE_LAG, j))
+            if u == GATE_AFTER:
+                for i, pos in enumerate((pos1, pos2, pos3, pos4)):
+                    nc.sync.dma_start(pos_sb[i][:], pos)
+                nc.sync.dma_start(out=gate_sb[:], in_=gate[:, 0:P, :].rearrange("i p t -> p i t"))
+            if u == WP_AFTER:
+                wp_raw = raws.tile([P, PACK, 512], F32, name="raw")
+                nc.sync.dma_start(out=wp_raw[:], in_=wp.rearrange("(p j) f -> p j f", j=PACK))
+            for when, j in list(due):
+                if when <= u and u < len(UNITS) - 1:
+                    combine(j)
+                    due.remove((when, j))
+        quantise(wp_raw, 0, wp_words, wp_bytes)
+        for when, j in due[:-1]:
+            combine(j)
+        t0 = 0
+        for nt in PIECES:
+            finish(due[-1][1], t0, nt, t0 + nt == T)
+            t0 += nt

@@ -20,12 +20,20 @@ RELU = mybir.ActivationFunctionType.Relu
 MULT = mybir.AluOpType.mult
 
 UNITS = [[(4 * g + q, j, 1) for q in range(4)] for j in range(4) for g in range(4)]
-VECTOR_COLS = [0] * 4 + [208] * 12
+VECTOR_COLS = [0] * 4 + [256, 384] + [160] * 10
 GATHER = 256
-PIECES = [256, 128, 128]
-GATE_AFTER = 2
-WP_AFTER = 13
-COMBINE_LAG = 2
+PIECES = [256,256]
+GATE_AFTER = 4
+WP_AFTER = 15
+BIAS_AT = {4: [0, 1], 5: [2, 3], 6: [4], 7: [5], 8: [6], 9: [7], 10: [8], 11: [9], 12: [10], 13: [11], 14: [12], 15: [13, 14, 15]}
+TAIL = ["sssv","vvsv"]
+WP_CUTS = [(0,128,"s"),(128,256,"s"),(256,384,"s"),(384,512,"s")]
+X_CUTS = [(0,128,"v"),(128,256,"s"),(256,384,"v"),(384,512,"s")]
+PROD_IN = [5,6,7,8, 9,10,11,12, 13,14,15,15]
+GATE_AT = [4,5,6,7]
+TAIL_ORDER = [0,1]
+LAST_CUTS = [(0,256),(256,256)]
+COMBINE_LAG = 1
 
 
 def interleave(copy, grouped, raw, c0, c1):
@@ -41,13 +49,32 @@ def tile_moe_nxt_lin_relu_kernel(
     nc = tc.nc
     with ExitStack() as ctx:
         keep = ctx.enter_context(tc.tile_pool(name="keep", bufs=1))
-        raws = ctx.enter_context(tc.tile_pool(name="raws", bufs=10))
-        work = ctx.enter_context(tc.tile_pool(name="work", bufs=4))
-        prods = ctx.enter_context(tc.tile_pool(name="prods", bufs=8))
-        psum = ctx.enter_context(tc.psum_pool(name="psum", bufs=8))
+        psum = ctx.enter_context(tc.psum_pool(name="psum", bufs=1))
+
+        banks = [psum.tile([P, 512], F32, name="bank%d" % r) for r in range(8)]
+        turn = {}
+
+        def take(tiles, key):
+            turn[key] = turn.get(key, -1) + 1
+            return tiles[turn[key] % len(tiles)]
+
+        def tiles(name, count, shape, dtype):
+            return [keep.tile(shape, dtype, name="%s%d" % (name, r), align_bytes=64) for r in range(count)]
+
+        raw_ring = tiles("raw", 9, [P, PACK, 512], F32)
+        grouped_ring = tiles("grouped", 6, [P, 512, PACK], BF16)
+        words_ring = tiles("words", 4, [P, 512], U32)
+        scales_ring = tiles("scales", 4, [P, 512], U8)
+        prod_ring = tiles("prod", 8, [P, T], F32)
+        cbf_ring = tiles("c_bf", 3, [P, 256, PACK], BF16)
+        cw_ring = tiles("c_words", 3, [P, 256], U32)
+        cb_ring = tiles("c_bytes", 3, [P, 256], U8)
+        staged_ring = tiles("staged", 6, [P, 512], F32)
+
+        copies = {"v": nc.vector.tensor_copy, "s": nc.scalar.copy}
 
         def bank():
-            return psum.tile([P, 512], F32, name="bank")
+            return take(banks[0:4], "bank")
 
         x_raw = keep.tile([P, PACK, T], F32, name="x_raw")
         x_rows = xT.rearrange("(p j) t -> p j t", j=PACK)
@@ -61,9 +88,8 @@ def tile_moe_nxt_lin_relu_kernel(
         ident = keep.tile([P, P], F32, name="ident")
         make_identity(nc, ident[:])
         x_bf = keep.tile([P, T, PACK], BF16, name="x_bf", align_bytes=64)
-        interleave(nc.vector.tensor_copy, x_bf, x_raw, 0, 256)
-        interleave(nc.scalar.copy, x_bf, x_raw, 256, 384)
-        interleave(nc.vector.tensor_copy, x_bf, x_raw, 384, 512)
+        for c0, c1, eng in X_CUTS:
+            interleave(copies[eng], x_bf, x_raw, c0, c1)
         for h in range(2):
             nc.vector.quantize_mx(
                 out=x_words[:, h * 256:(h + 1) * 256].bitcast(FP8X4),
@@ -84,16 +110,17 @@ def tile_moe_nxt_lin_relu_kernel(
             nc.vector.tensor_copy(slot_words[:, cols], x_words[:].indirect(entries))
             nc.vector.tensor_copy(slot_bytes[:, cols], x_bytes[:].indirect(entries))
 
-        bias = keep.tile([P, PACK, E], F32, name="bias")
+        bias = [keep.tile([P, 4], F32, name="bias%d" % u) for u in range(len(UNITS))]
         y = [keep.tile([P, S], F32, name="y%d" % j) for j in range(4)]
         gate_sb = keep.tile([P, TOP, T], F32, name="gate_sb")
         pos_sb = [keep.tile([P, T // 16], U16, name="pos%d" % i) for i in range(TOP)]
-        cT = keep.tile([P, 4, 2, P, 2], BF16, name="cT")
+        last_grouped = grouped_ring[(len(UNITS) - 1) % len(grouped_ring)]
+        cT = last_grouped[:].rearrange("t c k -> t (c k)").rearrange("t (b u p e) -> t b u p e", b=4, u=2, e=2)
         wp_words = keep.tile([P, M], U32, name="wp_words", align_bytes=64)
         wp_bytes = keep.tile([P, M], U8, name="wp_bytes", align_bytes=64)
 
         def quantise(raw, vcols, words, scales):
-            grouped = work.tile([P, 512, PACK], BF16, name="grouped", align_bytes=64)
+            grouped = take(grouped_ring, "grouped")
             if vcols > 0:
                 interleave(nc.vector.tensor_copy, grouped, raw, 0, vcols)
             if vcols < 512:
@@ -102,8 +129,25 @@ def tile_moe_nxt_lin_relu_kernel(
                 out=words[:].bitcast(FP8X4), scales=scales[:], in_=grouped[:].rearrange("p c t -> p (c t)")
             )
 
+        wp_raw = keep.tile([P, PACK, M], F32, name="wp_raw")
+
+        def load_bias(u):
+            col = 0
+            for e, j0, nj in UNITS[u]:
+                if nj > 1:
+                    with nc.allow_non_contiguous_dma(reason="one bias column"):
+                        nc.sync.dma_start(
+                            out=bias[u][:, col:col + nj],
+                            in_=b[j0 * P:(j0 + nj) * P, e:e + 1].rearrange("(j p) e -> p (j e)", p=P),
+                        )
+                col += nj
+            if UNITS[u][0][2] == 1:
+                e, j0, nj = UNITS[u][0]
+                nc.sync.dma_start(out=bias[u][:], in_=b[j0 * P:(j0 + 1) * P, e:e + 4])
+
         def run_unit(u):
-            raw = raws.tile([P, PACK, 512], F32, name="raw")
+            raw = take(raw_ring, "raw")
+            raw_of[u] = raw
             col = 0
             for e, j0, nj in UNITS[u]:
                 nc.sync.dma_start(
@@ -111,12 +155,17 @@ def tile_moe_nxt_lin_relu_kernel(
                     in_=w[e].rearrange("(p j) n -> p j n", j=PACK)[:, :, j0 * P:(j0 + nj) * P],
                 )
                 col += nj * P
-            if u == 0:
-                nc.sync.dma_start(out=bias[:], in_=b.rearrange("(j p) e -> p j e", p=P))
+            if u == WP_AFTER:
+                nc.sync.dma_start(out=wp_raw[:], in_=wp.rearrange("(p j) f -> p j f", j=PACK))
+            if u in BIAS_AT:
+                for v in BIAS_AT[u]:
+                    load_bias(v)
+                    if v < u:
+                        empty_unit(v)
             for e, j0, nj in UNITS[u]:
                 gather_slots(e)
-            words = work.tile([P, 512], U32, name="words", align_bytes=64)
-            scales = work.tile([P, 512], U8, name="scales", align_bytes=64)
+            words = take(words_ring, "words")
+            scales = take(scales_ring, "scales")
             quantise(raw, VECTOR_COLS[u], words, scales)
             acc = bank()
             parts = [(e, j) for e, j0, nj in UNITS[u] for j in range(j0, j0 + nj)]
@@ -129,51 +178,40 @@ def tile_moe_nxt_lin_relu_kernel(
                     rhs=slot_words[:, slots].bitcast(FP8X4), rhs_scale=slot_bytes[:, slots],
                     start=True, stop=True,
                 )
+            return acc, parts
+
+        def empty_unit(u):
+            acc, parts = sums[u]
             for q, (e, j) in enumerate(parts):
                 nc.scalar.activation(
-                    y[j][:, e * C:(e + 1) * C], acc[:, q * P:(q + 1) * P], RELU, bias=bias[:, j, e:e + 1]
+                    y[j][:, e * C:(e + 1) * C], acc[:, q * P:(q + 1) * P], RELU, bias=bias[u][:, q:q + 1]
                 )
-            return parts
 
-        def products(j, t0, nt):
-            made = []
-            for i in range(TOP):
-                prod = prods.tile([P, T], F32, name="prod")
-                nc.vector.tensor_tensor(
-                    prod[:, 0:nt],
-                    y[j][:].indirect(pos_sb[i][:, t0 // 16:(t0 + nt) // 16]),
-                    gate_sb[:, i, t0:t0 + nt],
-                    MULT,
+        def product(j, i, t0, nt, prod):
+            nc.vector.tensor_tensor(
+                prod[:, 0:nt],
+                y[j][:].indirect(pos_sb[i][:, t0 // 16:(t0 + nt) // 16]),
+                gate_sb[:, i, t0:t0 + nt],
+                MULT,
+            )
+            for blk in range(nt // P):
+                nc.tensor.matmul(
+                    banks[4 + t0 // P + blk][:, j * P:(j + 1) * P], prod[:, blk * P:(blk + 1) * P], ident[:],
+                    start=(i == 0), stop=(i == TOP - 1), is_transpose=True,
                 )
-                made.append(prod)
-            return made
 
-        def round_sums(copy, acc, j, blk0, nblk):
+        def round_sums(copy, blk, j0, nj):
             copy(
-                cT[:, blk0:blk0 + nblk, :, 32 * j:32 * (j + 1), :].rearrange("t b u p e -> t u b p e"),
-                acc[:, 0:nblk * P].rearrange("t (b p u e) -> t u b p e", b=nblk, u=2, e=2),
+                cT[:, blk, :, 32 * j0:32 * (j0 + nj), :],
+                banks[4 + blk][:, j0 * P:(j0 + nj) * P].rearrange("t (p u e) -> t u p e", u=2, e=2),
             )
 
-        def combine(j):
-            made = products(j, 0, T)
-            acc = bank()
-            for blk in range(4):
-                cols = slice(blk * P, (blk + 1) * P)
-                for i in range(TOP):
-                    nc.tensor.matmul(acc[:, cols], made[i][:, cols], ident[:], start=(i == 0), stop=(i == TOP - 1), is_transpose=True)
-            round_sums(nc.scalar.copy, acc, j, 0, 4)
-
-        def finish(j, t0, nt, last):
-            made = products(j, t0, nt)
+        def finish(j, t0, nt, how):
             nblk = nt // P
-            accs = [bank() for blk in range(nblk)]
-            for i in range(TOP):
-                for blk in range(nblk):
-                    nc.tensor.matmul(accs[blk][:, 0:P], made[i][:, blk * P:(blk + 1) * P], ident[:], start=(i == 0), stop=(i == TOP - 1), is_transpose=True)
-            c_bf = work.tile([P, 256, PACK], BF16, name="c_bf", align_bytes=64)
+            c_bf = take(cbf_ring, "cbf")
             for blk in range(nblk):
                 tb = t0 // P + blk
-                round_sums(nc.scalar.copy, accs[blk], j, tb, 1)
+                round_sums(copies[how[0]], tb, j, 1)
                 turned = bank()
                 for u in range(2):
                     nc.tensor.transpose(
@@ -181,12 +219,12 @@ def tile_moe_nxt_lin_relu_kernel(
                         cT[:, tb, u, :, :].rearrange("t p e -> t (p e)").bitcast(F32),
                         ident[:],
                     )
-                nc.scalar.copy(
+                copies[how[1]](
                     c_bf[:, blk * P:(blk + 1) * P, :].rearrange("p t k -> p (t k)").bitcast(F32).rearrange("p (t u) -> p t u", u=2),
                     turned[:, 0:2 * P].rearrange("p (u t) -> p t u", u=2),
                 )
-            c_words = work.tile([P, 256], U32, name="c_words", align_bytes=64)
-            c_bytes = work.tile([P, 256], U8, name="c_bytes", align_bytes=64)
+            c_words = take(cw_ring, "cw")
+            c_bytes = take(cb_ring, "cb")
             nc.vector.quantize_mx(
                 out=c_words[:, 0:nt].bitcast(FP8X4), scales=c_bytes[:, 0:nt],
                 in_=c_bf[:, 0:nt, :].rearrange("p t k -> p (t k)"),
@@ -201,38 +239,42 @@ def tile_moe_nxt_lin_relu_kernel(
                         rhs=c_words[:, 0:nt].bitcast(FP8X4), rhs_scale=c_bytes[:, 0:nt],
                         start=True, stop=True,
                     )
-                staged = work.tile([P, 512], F32, name="staged")
-                if last and half == 1:
-                    nc.vector.tensor_copy(staged[:, 0:2 * nt], res[:, 0:2 * nt])
-                else:
-                    nc.scalar.copy(staged[:, 0:2 * nt], res[:, 0:2 * nt])
+                staged = take(staged_ring, "staged")
+                copies[how[2 + half]](staged[:, 0:2 * nt], res[:, 0:2 * nt])
                 nc.sync.dma_start(
                     out=out[half * 256:(half + 1) * 256, t0:t0 + nt].rearrange("(q p) t -> p q t", p=P),
                     in_=staged[:, 0:2 * nt].rearrange("p (q t) -> p q t", q=2),
                 )
 
-        done = [0, 0, 0, 0]
-        due = []
-        for u in range(len(UNITS)):
-            for e, j in run_unit(u):
-                done[j] += 1
-                if done[j] == E:
-                    due.append((u + COMBINE_LAG, j))
-            if u == GATE_AFTER:
-                for i, pos in enumerate((pos1, pos2, pos3, pos4)):
-                    nc.sync.dma_start(pos_sb[i][:], pos)
-                nc.sync.dma_start(out=gate_sb[:], in_=gate[:, 0:P, :].rearrange("i p t -> p i t"))
+        sums = {}
+        raw_of = {}
+        used = {}
+        last = len(UNITS) - 1
+        for u in range(len(UNITS) + COMBINE_LAG):
+            if u <= last:
+                sums[u] = run_unit(u)
+            if u == last:
+                empty_unit(u)
+            for i in range(TOP):
+                if GATE_AT[i] == u:
+                    nc.sync.dma_start(pos_sb[i][:], (pos1, pos2, pos3, pos4)[i])
+                    nc.sync.dma_start(out=gate_sb[:, i, :], in_=gate[i, 0:P, :])
+            for q, v in enumerate(PROD_IN):
+                if v + COMBINE_LAG == u:
+                    used[v] = used.get(v, -1) + 1
+                    product(q // TOP, q % TOP, 0, T, raw_of[v][:, used[v], :])
             if u == WP_AFTER:
-                wp_raw = raws.tile([P, PACK, 512], F32, name="raw")
-                nc.sync.dma_start(out=wp_raw[:], in_=wp.rearrange("(p j) f -> p j f", j=PACK))
-            for when, j in list(due):
-                if when <= u and u < len(UNITS) - 1:
-                    combine(j)
-                    due.remove((when, j))
-        quantise(wp_raw, 0, wp_words, wp_bytes)
-        for when, j in due[:-1]:
-            combine(j)
-        t0 = 0
-        for nt in PIECES:
-            finish(due[-1][1], t0, nt, t0 + nt == T)
-            t0 += nt
+                wp_bf = keep.tile([P, 512, PACK], BF16, name="wp_bf", align_bytes=64)
+                for c0, c1, eng in WP_CUTS:
+                    interleave(copies[eng], wp_bf, wp_raw, c0, c1)
+                nc.vector.quantize_mx(
+                    out=wp_words[:].bitcast(FP8X4), scales=wp_bytes[:], in_=wp_bf[:].rearrange("p c t -> p (c t)")
+                )
+        for blk in range(4):
+            round_sums(nc.scalar.copy, blk, 0, 3)
+        starts = [sum(PIECES[:r]) for r in range(len(PIECES))]
+        for t0, nt in LAST_CUTS:
+            for i in range(TOP):
+                product(3, i, t0, nt, take(prod_ring, "prod"))
+        for r in TAIL_ORDER:
+            finish(3, starts[r], PIECES[r], TAIL[r])

@@ -19,21 +19,24 @@ FP8X4 = mybir.dt.float8_e4m3fn_x4
 RELU = mybir.ActivationFunctionType.Relu
 MULT = mybir.AluOpType.mult
 
-UNITS = [[(4 * g + q, j, 1) for q in range(4)] for j in range(4) for g in range(4)]
-VECTOR_COLS = [0] * 4 + [256, 384] + [160] * 10
-GATHER = 256
-PIECES = [256,256]
-GATE_AFTER = 4
-WP_AFTER = 15
-BIAS_AT = {4: [0, 1], 5: [2, 3], 6: [4], 7: [5], 8: [6], 9: [7], 10: [8], 11: [9], 12: [10], 13: [11], 14: [12], 15: [13, 14, 15]}
-TAIL = ["sssv","vvsv"]
-WP_CUTS = [(0,128,"s"),(128,256,"s"),(256,384,"s"),(384,512,"s")]
-X_CUTS = [(0,128,"v"),(128,256,"s"),(256,384,"v"),(384,512,"s")]
-PROD_IN = [5,6,7,8, 9,10,11,12, 13,14,15,15]
-GATE_AT = [4,5,6,7]
-TAIL_ORDER = [0,1]
-LAST_CUTS = [(0,256),(256,256)]
-COMBINE_LAG = 1
+UNITS = [[(0, 0, 4)], [(1, 0, 4)], [(2, 0, 4)], [(3, 0, 4)], [(4, 0, 4)], [(5, 0, 4)], [(6, 0, 4)], [(7, 0, 4)], [(8, 0, 1), (9, 0, 1)], [(10, 0, 1), (11, 0, 1)], [(12, 0, 1), (13, 0, 1)], [(14, 0, 1), (15, 0, 1)], [(8, 1, 1), (9, 1, 1)], [(10, 1, 1), (11, 1, 1)], [(12, 1, 1), (13, 1, 1)], [(14, 1, 1), (15, 1, 1)], [(8, 2, 1), (9, 2, 1)], [(10, 2, 1), (11, 2, 1)], [(12, 2, 1), (13, 2, 1)], [(14, 2, 1), (15, 2, 1)], [(8, 3, 1), (9, 3, 1)], [(10, 3, 1), (11, 3, 1)], [(12, 3, 1), (13, 3, 1)], [(14, 3, 1), (15, 3, 1)]]
+VECTOR_COLS = [0, 0, 256, 0, 384, 384, 384, 384, 128, 128, 0, 192, 0, 0, 0, 0, 0, 0, 128, 0, 0, 0, 0, 0]
+BANK_OF = [4, 5, 6, 7, 0, 1, 2, 3, 4, 5, 6, 7, 0, 1, 2, 3, 0, 1, 2, 3, 0, 1, 2, 3]
+BIAS_LOADS = [(5, 0, 4, 0, 4), (6, 4, 2, 0, 4), (8, 6, 2, 0, 4), (9, 8, 2, 0, 1), (10, 10, 2, 0, 1), (11, 12, 2, 0, 1), (12, 14, 2, 0, 1), (13, 8, 2, 1, 1), (14, 10, 2, 1, 1), (15, 12, 2, 1, 1), (16, 14, 2, 1, 1), (17, 8, 2, 2, 1), (18, 10, 2, 2, 1), (20, 12, 2, 2, 1), (20, 14, 2, 2, 1), (22, 8, 2, 3, 1), (22, 10, 2, 3, 1), (23, 12, 2, 3, 1), (23, 14, 2, 3, 1)]
+EMPTY_AFTER = {5: [(0, 0), (1, 0), (2, 0), (3, 0), (0, 1), (1, 1), (2, 1), (3, 1), (0, 2), (1, 2), (2, 2), (3, 2), (0, 3), (1, 3), (2, 3), (3, 3)], 6: [(4, 0), (5, 0), (4, 1), (5, 1), (4, 2), (5, 2), (4, 3), (5, 3)], 8: [(6, 0), (7, 0), (6, 1), (7, 1), (6, 2), (7, 2), (6, 3), (7, 3)], 9: [(8, 0), (9, 0)], 10: [(10, 0), (11, 0)], 11: [(12, 0), (13, 0)], 12: [(14, 0), (15, 0)], 13: [(8, 1), (9, 1)], 14: [(10, 1), (11, 1)], 15: [(12, 1), (13, 1)], 16: [(14, 1), (15, 1)], 17: [(8, 2), (9, 2)], 18: [(10, 2), (11, 2)], 20: [(12, 2), (13, 2), (14, 2), (15, 2)], 22: [(8, 3), (9, 3), (10, 3), (11, 3)], 23: [(12, 3), (13, 3), (14, 3), (15, 3)]}
+GATHER = 384
+PIECES = [256, 128, 128]
+LAST_CUTS = [[0, 256], [256, 128], [384, 128]]
+TAIL = ['vsss', 'vsss', 'svss']
+TAIL_ORDER = [('g', 0), ('t', 0), ('g', 1), ('t', 1), ('p', 0), ('g', 2), ('t', 2), ('p', 1), ('p', 2)]
+WP_AFTER = 23
+WP_TEXT = 23
+WP_CUTS = [(0, 256, 's'), (256, 512, 's')]
+X_LOADS = [[0, 512]]
+X_CUTS = [[0, 256, 'v'], [256, 512, 's']]
+PROD_IN = [(12, 15), (13, 15), (14, 15), (15, 15), (16, 19), (17, 19), (18, 19), (19, 19), (20, 20), (21, 23), (22, 23), (23, 23)]
+GATE_AT = [3, 3, 3, 3]
+COMBINE_LAG = 0
 
 
 def interleave(copy, grouped, raw, c0, c1):
@@ -50,13 +53,12 @@ def tile_moe_nxt_lin_relu_kernel(
     with ExitStack() as ctx:
         keep = ctx.enter_context(tc.tile_pool(name="keep", bufs=1))
         psum = ctx.enter_context(tc.psum_pool(name="psum", bufs=1))
-
         banks = [psum.tile([P, 512], F32, name="bank%d" % r) for r in range(8)]
         turn = {}
 
-        def take(tiles, key):
+        def take(ring, key):
             turn[key] = turn.get(key, -1) + 1
-            return tiles[turn[key] % len(tiles)]
+            return ring[turn[key] % len(ring)]
 
         def tiles(name, count, shape, dtype):
             return [keep.tile(shape, dtype, name="%s%d" % (name, r), align_bytes=64) for r in range(count)]
@@ -66,20 +68,21 @@ def tile_moe_nxt_lin_relu_kernel(
         words_ring = tiles("words", 4, [P, 512], U32)
         scales_ring = tiles("scales", 4, [P, 512], U8)
         prod_ring = tiles("prod", 8, [P, T], F32)
-        cbf_ring = tiles("c_bf", 3, [P, 256, PACK], BF16)
-        cw_ring = tiles("c_words", 3, [P, 256], U32)
-        cb_ring = tiles("c_bytes", 3, [P, 256], U8)
-        staged_ring = tiles("staged", 6, [P, 512], F32)
-
+        cbf_ring = tiles("c_bf", 4, [P, 256, PACK], BF16)
+        cw_ring = tiles("c_words", 4, [P, 256], U32)
+        cb_ring = tiles("c_bytes", 4, [P, 256], U8)
+        staged_ring = tiles("staged", 8, [P, 512], F32)
         copies = {"v": nc.vector.tensor_copy, "s": nc.scalar.copy}
 
         def bank():
             return take(banks[0:4], "bank")
 
+        gate_rows = keep.tile([P, T], F32, name="gate_rows")
+        nc.gpsimd.memset(gate_rows[:], 0.0)
         x_raw = keep.tile([P, PACK, T], F32, name="x_raw")
         x_rows = xT.rearrange("(p j) t -> p j t", j=PACK)
-        for h in range(2):
-            nc.sync.dma_start(out=x_raw[:, :, h * 256:(h + 1) * 256], in_=x_rows[:, :, h * 256:(h + 1) * 256])
+        for c0, c1 in X_LOADS:
+            nc.sync.dma_start(out=x_raw[:, :, c0:c1], in_=x_rows[:, :, c0:c1])
         offs_sb = keep.tile([P, S // 16], U16, name="offs_sb")
         nc.sync.dma_start(offs_sb[:], offs)
         x_words = keep.tile([P, T], U32, name="x_words", align_bytes=64)
@@ -87,6 +90,8 @@ def tile_moe_nxt_lin_relu_kernel(
         nc.gpsimd.memset(x_bytes[:], 0)
         ident = keep.tile([P, P], F32, name="ident")
         make_identity(nc, ident[:])
+        gate_sb = keep.tile([P, TOP, T], F32, name="gate_sb")
+        nc.sync.dma_start(out=gate_rows[0:TOP, :], in_=gate[:, 0, :])
         x_bf = keep.tile([P, T, PACK], BF16, name="x_bf", align_bytes=64)
         for c0, c1, eng in X_CUTS:
             interleave(copies[eng], x_bf, x_raw, c0, c1)
@@ -98,52 +103,34 @@ def tile_moe_nxt_lin_relu_kernel(
             )
         slot_words = keep.tile([P, S], U32, name="slot_words", align_bytes=64)
         slot_bytes = keep.tile([P, S], U8, name="slot_bytes", align_bytes=64)
-        gathered = set()
-
-        def gather_slots(e):
-            g = e * C // GATHER
-            if g in gathered:
-                return
-            gathered.add(g)
-            cols = slice(g * GATHER, (g + 1) * GATHER)
-            entries = offs_sb[:, g * GATHER // 16:(g + 1) * GATHER // 16]
+        for s0 in range(0, S, GATHER):
+            cols = slice(s0, min(S, s0 + GATHER))
+            entries = offs_sb[:, cols.start // 16:cols.stop // 16]
             nc.vector.tensor_copy(slot_words[:, cols], x_words[:].indirect(entries))
             nc.vector.tensor_copy(slot_bytes[:, cols], x_bytes[:].indirect(entries))
 
-        bias = [keep.tile([P, 4], F32, name="bias%d" % u) for u in range(len(UNITS))]
+        for blk in range(4):
+            nc.tensor.transpose(banks[4][:, blk * P:(blk + 1) * P], gate_rows[:, blk * P:(blk + 1) * P], ident[:])
+        gate_cols = keep.tile([P, 4, TOP], F32, name="gate_cols")
+        nc.scalar.copy(gate_cols[:], banks[4][:].rearrange("t (b r) -> t b r", b=4)[:, :, 0:TOP])
+        for i in range(TOP):
+            for blk in range(4):
+                nc.tensor.transpose(
+                    banks[i][:, blk * P:(blk + 1) * P], gate_cols[:, blk, i:i + 1].to_broadcast([P, P]), ident[:]
+                )
+            copies['ssss'[i]](gate_sb[:, i, :], banks[i][:])
+
         y = [keep.tile([P, S], F32, name="y%d" % j) for j in range(4)]
-        gate_sb = keep.tile([P, TOP, T], F32, name="gate_sb")
         pos_sb = [keep.tile([P, T // 16], U16, name="pos%d" % i) for i in range(TOP)]
         last_grouped = grouped_ring[(len(UNITS) - 1) % len(grouped_ring)]
         cT = last_grouped[:].rearrange("t c k -> t (c k)").rearrange("t (b u p e) -> t b u p e", b=4, u=2, e=2)
+        wp_raw = keep.tile([P, PACK, M], F32, name="wp_raw")
+        wp_bf = keep.tile([P, M, PACK], BF16, name="wp_bf", align_bytes=64)
         wp_words = keep.tile([P, M], U32, name="wp_words", align_bytes=64)
         wp_bytes = keep.tile([P, M], U8, name="wp_bytes", align_bytes=64)
-
-        def quantise(raw, vcols, words, scales):
-            grouped = take(grouped_ring, "grouped")
-            if vcols > 0:
-                interleave(nc.vector.tensor_copy, grouped, raw, 0, vcols)
-            if vcols < 512:
-                interleave(nc.scalar.copy, grouped, raw, vcols, 512)
-            nc.vector.quantize_mx(
-                out=words[:].bitcast(FP8X4), scales=scales[:], in_=grouped[:].rearrange("p c t -> p (c t)")
-            )
-
-        wp_raw = keep.tile([P, PACK, M], F32, name="wp_raw")
-
-        def load_bias(u):
-            col = 0
-            for e, j0, nj in UNITS[u]:
-                if nj > 1:
-                    with nc.allow_non_contiguous_dma(reason="one bias column"):
-                        nc.sync.dma_start(
-                            out=bias[u][:, col:col + nj],
-                            in_=b[j0 * P:(j0 + nj) * P, e:e + 1].rearrange("(j p) e -> p (j e)", p=P),
-                        )
-                col += nj
-            if UNITS[u][0][2] == 1:
-                e, j0, nj = UNITS[u][0]
-                nc.sync.dma_start(out=bias[u][:], in_=b[j0 * P:(j0 + 1) * P, e:e + 4])
+        bias = {}
+        sums = {}
+        raw_of = {}
 
         def run_unit(u):
             raw = take(raw_ring, "raw")
@@ -155,36 +142,39 @@ def tile_moe_nxt_lin_relu_kernel(
                     in_=w[e].rearrange("(p j) n -> p j n", j=PACK)[:, :, j0 * P:(j0 + nj) * P],
                 )
                 col += nj * P
+            for at, e0, ne, j0, nj in BIAS_LOADS:
+                if at == u:
+                    part = keep.tile([P, nj, ne], F32, name="bias_%d_%d" % (e0, j0))
+                    with nc.allow_non_contiguous_dma(reason="a few bias columns"):
+                        nc.sync.dma_start(
+                            out=part[:], in_=b[j0 * P:(j0 + nj) * P, e0:e0 + ne].rearrange("(j p) e -> p j e", p=P)
+                        )
+                    for e in range(ne):
+                        for j in range(nj):
+                            bias[(e0 + e, j0 + j)] = part[:, j, e:e + 1]
             if u == WP_AFTER:
                 nc.sync.dma_start(out=wp_raw[:], in_=wp.rearrange("(p j) f -> p j f", j=PACK))
-            if u in BIAS_AT:
-                for v in BIAS_AT[u]:
-                    load_bias(v)
-                    if v < u:
-                        empty_unit(v)
-            for e, j0, nj in UNITS[u]:
-                gather_slots(e)
+            grouped = take(grouped_ring, "grouped")
+            if VECTOR_COLS[u] > 0:
+                interleave(nc.vector.tensor_copy, grouped, raw, 0, VECTOR_COLS[u])
+            if VECTOR_COLS[u] < col:
+                interleave(nc.scalar.copy, grouped, raw, VECTOR_COLS[u], col)
             words = take(words_ring, "words")
             scales = take(scales_ring, "scales")
-            quantise(raw, VECTOR_COLS[u], words, scales)
-            acc = bank()
+            nc.vector.quantize_mx(
+                out=words[:, 0:col].bitcast(FP8X4), scales=scales[:, 0:col],
+                in_=grouped[:, 0:col, :].rearrange("p c t -> p (c t)"),
+            )
             parts = [(e, j) for e, j0, nj in UNITS[u] for j in range(j0, j0 + nj)]
             for q, (e, j) in enumerate(parts):
                 cols = slice(q * P, (q + 1) * P)
                 slots = slice(e * C, (e + 1) * C)
+                sums[(e, j)] = banks[BANK_OF[u]][:, cols]
                 nc.tensor.matmul_mx(
-                    out=acc[:, cols],
+                    out=sums[(e, j)],
                     lhsT=words[:, cols].bitcast(FP8X4), lhsT_scale=scales[:, cols],
                     rhs=slot_words[:, slots].bitcast(FP8X4), rhs_scale=slot_bytes[:, slots],
                     start=True, stop=True,
-                )
-            return acc, parts
-
-        def empty_unit(u):
-            acc, parts = sums[u]
-            for q, (e, j) in enumerate(parts):
-                nc.scalar.activation(
-                    y[j][:, e * C:(e + 1) * C], acc[:, q * P:(q + 1) * P], RELU, bias=bias[u][:, q:q + 1]
                 )
 
         def product(j, i, t0, nt, prod):
@@ -206,9 +196,12 @@ def tile_moe_nxt_lin_relu_kernel(
                 banks[4 + blk][:, j0 * P:(j0 + nj) * P].rearrange("t (p u e) -> t u p e", u=2, e=2),
             )
 
-        def finish(j, t0, nt, how):
+        rounded = {}
+
+        def turn_piece(j, t0, nt, how):
             nblk = nt // P
             c_bf = take(cbf_ring, "cbf")
+            rounded[t0] = c_bf
             for blk in range(nblk):
                 tb = t0 // P + blk
                 round_sums(copies[how[0]], tb, j, 1)
@@ -223,6 +216,9 @@ def tile_moe_nxt_lin_relu_kernel(
                     c_bf[:, blk * P:(blk + 1) * P, :].rearrange("p t k -> p (t k)").bitcast(F32).rearrange("p (t u) -> p t u", u=2),
                     turned[:, 0:2 * P].rearrange("p (u t) -> p t u", u=2),
                 )
+
+        def project(t0, nt, how):
+            c_bf = rounded[t0]
             c_words = take(cw_ring, "cw")
             c_bytes = take(cb_ring, "cb")
             nc.vector.quantize_mx(
@@ -246,25 +242,20 @@ def tile_moe_nxt_lin_relu_kernel(
                     in_=staged[:, 0:2 * nt].rearrange("p (q t) -> p q t", q=2),
                 )
 
-        sums = {}
-        raw_of = {}
         used = {}
-        last = len(UNITS) - 1
         for u in range(len(UNITS) + COMBINE_LAG):
-            if u <= last:
-                sums[u] = run_unit(u)
-            if u == last:
-                empty_unit(u)
+            if u < len(UNITS):
+                run_unit(u)
+            for e, j in EMPTY_AFTER.get(u, []):
+                nc.scalar.activation(y[j][:, e * C:(e + 1) * C], sums[(e, j)], RELU, bias=bias[(e, j)])
             for i in range(TOP):
                 if GATE_AT[i] == u:
                     nc.sync.dma_start(pos_sb[i][:], (pos1, pos2, pos3, pos4)[i])
-                    nc.sync.dma_start(out=gate_sb[:, i, :], in_=gate[i, 0:P, :])
-            for q, v in enumerate(PROD_IN):
-                if v + COMBINE_LAG == u:
+            for q, (v, at) in enumerate(PROD_IN):
+                if at == u:
                     used[v] = used.get(v, -1) + 1
-                    product(q // TOP, q % TOP, 0, T, raw_of[v][:, used[v], :])
-            if u == WP_AFTER:
-                wp_bf = keep.tile([P, 512, PACK], BF16, name="wp_bf", align_bytes=64)
+                    product(q // TOP, q % TOP, 0, T, raw_of[v][:, used[v], :] if v >= 0 else take(prod_ring, "prod"))
+            if u == WP_TEXT:
                 for c0, c1, eng in WP_CUTS:
                     interleave(copies[eng], wp_bf, wp_raw, c0, c1)
                 nc.vector.quantize_mx(
@@ -273,8 +264,11 @@ def tile_moe_nxt_lin_relu_kernel(
         for blk in range(4):
             round_sums(nc.scalar.copy, blk, 0, 3)
         starts = [sum(PIECES[:r]) for r in range(len(PIECES))]
-        for t0, nt in LAST_CUTS:
-            for i in range(TOP):
-                product(3, i, t0, nt, take(prod_ring, "prod"))
-        for r in TAIL_ORDER:
-            finish(3, starts[r], PIECES[r], TAIL[r])
+        for what, r in TAIL_ORDER:
+            if what == "g":
+                for i in range(TOP):
+                    product(3, i, LAST_CUTS[r][0], LAST_CUTS[r][1], take(prod_ring, "prod"))
+            elif what == "t":
+                turn_piece(3, starts[r], PIECES[r], TAIL[r])
+            else:
+                project(starts[r], PIECES[r], TAIL[r])

@@ -7,8 +7,10 @@ K, T, E, C, N, M, TOP = 512, 512, 16, 128, 512, 512, 4
 S = E * C
 P = 128
 PACK = 4
+TILES = N // P
+BLOCKS = T // P
 FLOPS = 2 * K * N * S + 2 * N * M * T
-BYTES = 4 * (K * T + E * K * N + N * E + N * M + TOP * P * T + M * T) + 2 * P * (S + TOP * T) // 16
+BYTES = 4 * (K * T + E * K * N + N * E + N * M + TOP * T + M * T) + 2 * P * (S + TOP * T) // 16
 
 F32 = mybir.dt.float32
 BF16 = mybir.dt.bfloat16
@@ -19,31 +21,63 @@ FP8X4 = mybir.dt.float8_e4m3fn_x4
 RELU = mybir.ActivationFunctionType.Relu
 MULT = mybir.AluOpType.mult
 
-UNITS = [[(0, 0, 4)], [(1, 0, 4)], [(2, 0, 4)], [(3, 0, 4)], [(4, 0, 4)], [(5, 0, 4)], [(6, 0, 4)], [(7, 0, 4)], [(8, 0, 1), (9, 0, 1)], [(10, 0, 1), (11, 0, 1)], [(12, 0, 1), (13, 0, 1)], [(14, 0, 1), (15, 0, 1)], [(8, 1, 1), (9, 1, 1)], [(10, 1, 1), (11, 1, 1)], [(12, 1, 1), (13, 1, 1)], [(14, 1, 1), (15, 1, 1)], [(8, 2, 1), (9, 2, 1)], [(10, 2, 1), (11, 2, 1)], [(12, 2, 1), (13, 2, 1)], [(14, 2, 1), (15, 2, 1)], [(8, 3, 1), (9, 3, 1)], [(10, 3, 1), (11, 3, 1)], [(12, 3, 1), (13, 3, 1)], [(14, 3, 1), (15, 3, 1)]]
-VECTOR_COLS = [0, 0, 256, 0, 384, 384, 384, 384, 128, 128, 0, 192, 0, 0, 0, 0, 0, 0, 128, 0, 0, 0, 0, 0]
-BANK_OF = [4, 5, 6, 7, 0, 1, 2, 3, 4, 5, 6, 7, 0, 1, 2, 3, 0, 1, 2, 3, 0, 1, 2, 3]
-BIAS_LOADS = [(5, 0, 4, 0, 4), (6, 4, 2, 0, 4), (8, 6, 2, 0, 4), (9, 8, 2, 0, 1), (10, 10, 2, 0, 1), (11, 12, 2, 0, 1), (12, 14, 2, 0, 1), (13, 8, 2, 1, 1), (14, 10, 2, 1, 1), (15, 12, 2, 1, 1), (16, 14, 2, 1, 1), (17, 8, 2, 2, 1), (18, 10, 2, 2, 1), (20, 12, 2, 2, 1), (20, 14, 2, 2, 1), (22, 8, 2, 3, 1), (22, 10, 2, 3, 1), (23, 12, 2, 3, 1), (23, 14, 2, 3, 1)]
-EMPTY_AFTER = {5: [(0, 0), (1, 0), (2, 0), (3, 0), (0, 1), (1, 1), (2, 1), (3, 1), (0, 2), (1, 2), (2, 2), (3, 2), (0, 3), (1, 3), (2, 3), (3, 3)], 6: [(4, 0), (5, 0), (4, 1), (5, 1), (4, 2), (5, 2), (4, 3), (5, 3)], 8: [(6, 0), (7, 0), (6, 1), (7, 1), (6, 2), (7, 2), (6, 3), (7, 3)], 9: [(8, 0), (9, 0)], 10: [(10, 0), (11, 0)], 11: [(12, 0), (13, 0)], 12: [(14, 0), (15, 0)], 13: [(8, 1), (9, 1)], 14: [(10, 1), (11, 1)], 15: [(12, 1), (13, 1)], 16: [(14, 1), (15, 1)], 17: [(8, 2), (9, 2)], 18: [(10, 2), (11, 2)], 20: [(12, 2), (13, 2), (14, 2), (15, 2)], 22: [(8, 3), (9, 3), (10, 3), (11, 3)], 23: [(12, 3), (13, 3), (14, 3), (15, 3)]}
-GATHER = 384
-PIECES = [256, 128, 128]
-LAST_CUTS = [[0, 256], [256, 128], [384, 128]]
-TAIL = ['vsss', 'vsss', 'svss']
-TAIL_ORDER = [('g', 0), ('t', 0), ('g', 1), ('t', 1), ('p', 0), ('g', 2), ('t', 2), ('p', 1), ('p', 2)]
-WP_AFTER = 23
-WP_TEXT = 23
-WP_CUTS = [(0, 256, 's'), (256, 512, 's')]
-X_LOADS = [[0, 512]]
-X_CUTS = [[0, 256, 'v'], [256, 512, 's']]
-PROD_IN = [(12, 15), (13, 15), (14, 15), (15, 15), (16, 19), (17, 19), (18, 19), (19, 19), (20, 20), (21, 23), (22, 23), (23, 23)]
-GATE_AT = [3, 3, 3, 3]
-COMBINE_LAG = 0
+SPLIT = 8
+WHOLE = E - SPLIT
+PAIRS = SPLIT // 2
+UNITS = [[(e, 0, TILES)] for e in range(WHOLE)] + [
+    [(e, j, 1), (e + 1, j, 1)] for j in range(TILES) for e in range(WHOLE, E, 2)
+]
+LAST_UNIT = len(UNITS) - 1
+
+VECTOR_COLS = (
+    [0, 0, 512, 0, 0, 256, 512, 512]
+    + [128, 128, 256, 256]
+    + [256, 64, 0, 0]
+    + [64, 0, 0, 0]
+    + [64, 0, 0, 0]
+)
+WP_SCALAR_CUTS = [(0, 256), (256, 384)]
+HALF = T // 2
+
+FIRST_EXPERTS = 4
+FIRST_BIAS_UNIT = 5
+LISTS_UNIT = 3
+TOKEN_GATHER = 384
+
+RAW_TILES = 9
+ROUNDED_TILES = 6
+QUANTISED_TILES = 4
+UNIT_BANKS = 4
 
 
-def interleave(copy, grouped, raw, c0, c1):
+def interleave(copy, rounded, raw, c0, c1):
     copy(
-        grouped[:, c0:c1, :].rearrange("p (c i) t -> p c t i", i=2),
-        raw[:, :, c0:c1].rearrange("p t (c i) -> p c t i", i=2),
+        rounded[:, c0:c1, :].rearrange("p (c i) r -> p c r i", i=2),
+        raw[:, :, c0:c1].rearrange("p r (c i) -> p c r i", i=2),
     )
+
+
+def quantise(nc, words, scales, rounded):
+    nc.vector.quantize_mx(out=words.bitcast(FP8X4), scales=scales, in_=rounded.rearrange("p c r -> p (c r)"))
+
+
+def multiply(nc, result, left_words, left_scales, right_words, right_scales):
+    nc.tensor.matmul_mx(
+        out=result,
+        lhsT=left_words.bitcast(FP8X4), lhsT_scale=left_scales,
+        rhs=right_words.bitcast(FP8X4), rhs_scale=right_scales,
+        start=True, stop=True,
+    )
+
+
+def sums_read_after(u):
+    if u == FIRST_BIAS_UNIT:
+        return [(e, j) for j in range(TILES) for e in range(FIRST_EXPERTS)]
+    if u == WHOLE - 1:
+        return [(e, j) for j in range(TILES) for e in range(FIRST_EXPERTS, WHOLE)]
+    if u >= WHOLE:
+        return [(e, j) for e, j, tiles in UNITS[u]]
+    return []
 
 
 def tile_moe_nxt_lin_relu_kernel(
@@ -54,221 +88,190 @@ def tile_moe_nxt_lin_relu_kernel(
         keep = ctx.enter_context(tc.tile_pool(name="keep", bufs=1))
         psum = ctx.enter_context(tc.psum_pool(name="psum", bufs=1))
         banks = [psum.tile([P, 512], F32, name="bank%d" % r) for r in range(8)]
-        turn = {}
-
-        def take(ring, key):
-            turn[key] = turn.get(key, -1) + 1
-            return ring[turn[key] % len(ring)]
+        c_banks = banks[UNIT_BANKS:]
 
         def tiles(name, count, shape, dtype):
             return [keep.tile(shape, dtype, name="%s%d" % (name, r), align_bytes=64) for r in range(count)]
 
-        raw_ring = tiles("raw", 9, [P, PACK, 512], F32)
-        grouped_ring = tiles("grouped", 6, [P, 512, PACK], BF16)
-        words_ring = tiles("words", 4, [P, 512], U32)
-        scales_ring = tiles("scales", 4, [P, 512], U8)
-        prod_ring = tiles("prod", 8, [P, T], F32)
-        cbf_ring = tiles("c_bf", 4, [P, 256, PACK], BF16)
-        cw_ring = tiles("c_words", 4, [P, 256], U32)
-        cb_ring = tiles("c_bytes", 4, [P, 256], U8)
-        staged_ring = tiles("staged", 8, [P, 512], F32)
-        copies = {"v": nc.vector.tensor_copy, "s": nc.scalar.copy}
-
-        def bank():
-            return take(banks[0:4], "bank")
+        raw_tiles = tiles("raw", RAW_TILES, [P, PACK, N], F32)
+        rounded_tiles = tiles("rounded", ROUNDED_TILES, [P, N, PACK], BF16)
+        word_tiles = tiles("words", QUANTISED_TILES, [P, N], U32)
+        scale_tiles = tiles("scales", QUANTISED_TILES, [P, N], U8)
 
         gate_rows = keep.tile([P, T], F32, name="gate_rows")
         nc.gpsimd.memset(gate_rows[:], 0.0)
         x_raw = keep.tile([P, PACK, T], F32, name="x_raw")
-        x_rows = xT.rearrange("(p j) t -> p j t", j=PACK)
-        for c0, c1 in X_LOADS:
-            nc.sync.dma_start(out=x_raw[:, :, c0:c1], in_=x_rows[:, :, c0:c1])
+        nc.sync.dma_start(out=x_raw[:], in_=xT.rearrange("(p r) t -> p r t", r=PACK))
         offs_sb = keep.tile([P, S // 16], U16, name="offs_sb")
         nc.sync.dma_start(offs_sb[:], offs)
         x_words = keep.tile([P, T], U32, name="x_words", align_bytes=64)
-        x_bytes = keep.tile([P, T], U8, name="x_bytes", align_bytes=64)
-        nc.gpsimd.memset(x_bytes[:], 0)
+        x_scales = keep.tile([P, T], U8, name="x_scales", align_bytes=64)
+        nc.gpsimd.memset(x_scales[:], 0)
         ident = keep.tile([P, P], F32, name="ident")
         make_identity(nc, ident[:])
-        gate_sb = keep.tile([P, TOP, T], F32, name="gate_sb")
         nc.sync.dma_start(out=gate_rows[0:TOP, :], in_=gate[:, 0, :])
-        x_bf = keep.tile([P, T, PACK], BF16, name="x_bf", align_bytes=64)
-        for c0, c1, eng in X_CUTS:
-            interleave(copies[eng], x_bf, x_raw, c0, c1)
-        for h in range(2):
-            nc.vector.quantize_mx(
-                out=x_words[:, h * 256:(h + 1) * 256].bitcast(FP8X4),
-                scales=x_bytes[:, h * 256:(h + 1) * 256],
-                in_=x_bf[:, h * 256:(h + 1) * 256, :].rearrange("p c t -> p (c t)"),
-            )
+        x_rounded = keep.tile([P, T, PACK], BF16, name="x_rounded", align_bytes=64)
+        interleave(nc.vector.tensor_copy, x_rounded, x_raw, 0, HALF)
+        interleave(nc.scalar.copy, x_rounded, x_raw, HALF, T)
+        for t0 in (0, HALF):
+            tokens = slice(t0, t0 + HALF)
+            quantise(nc, x_words[:, tokens], x_scales[:, tokens], x_rounded[:, tokens, :])
         slot_words = keep.tile([P, S], U32, name="slot_words", align_bytes=64)
-        slot_bytes = keep.tile([P, S], U8, name="slot_bytes", align_bytes=64)
-        for s0 in range(0, S, GATHER):
-            cols = slice(s0, min(S, s0 + GATHER))
-            entries = offs_sb[:, cols.start // 16:cols.stop // 16]
-            nc.vector.tensor_copy(slot_words[:, cols], x_words[:].indirect(entries))
-            nc.vector.tensor_copy(slot_bytes[:, cols], x_bytes[:].indirect(entries))
+        slot_scales = keep.tile([P, S], U8, name="slot_scales", align_bytes=64)
+        for s0 in range(0, S, TOKEN_GATHER):
+            s1 = min(S, s0 + TOKEN_GATHER)
+            entries = offs_sb[:, s0 // 16:s1 // 16]
+            nc.vector.tensor_copy(slot_words[:, s0:s1], x_words[:].indirect(entries))
+            nc.vector.tensor_copy(slot_scales[:, s0:s1], x_scales[:].indirect(entries))
 
-        for blk in range(4):
-            nc.tensor.transpose(banks[4][:, blk * P:(blk + 1) * P], gate_rows[:, blk * P:(blk + 1) * P], ident[:])
-        gate_cols = keep.tile([P, 4, TOP], F32, name="gate_cols")
-        nc.scalar.copy(gate_cols[:], banks[4][:].rearrange("t (b r) -> t b r", b=4)[:, :, 0:TOP])
+        for blk in range(BLOCKS):
+            nc.tensor.transpose(c_banks[0][:, blk * P:(blk + 1) * P], gate_rows[:, blk * P:(blk + 1) * P], ident[:])
+        gate_cols = keep.tile([P, BLOCKS, TOP], F32, name="gate_cols")
+        nc.scalar.copy(gate_cols[:], c_banks[0][:].rearrange("t (b r) -> t b r", b=BLOCKS)[:, :, 0:TOP])
+        gate_sb = keep.tile([P, TOP, T], F32, name="gate_sb")
         for i in range(TOP):
-            for blk in range(4):
+            for blk in range(BLOCKS):
                 nc.tensor.transpose(
                     banks[i][:, blk * P:(blk + 1) * P], gate_cols[:, blk, i:i + 1].to_broadcast([P, P]), ident[:]
                 )
-            copies['ssss'[i]](gate_sb[:, i, :], banks[i][:])
+            nc.scalar.copy(gate_sb[:, i, :], banks[i][:])
 
-        y = [keep.tile([P, S], F32, name="y%d" % j) for j in range(4)]
+        y = [keep.tile([P, S], F32, name="y%d" % j) for j in range(TILES)]
         pos_sb = [keep.tile([P, T // 16], U16, name="pos%d" % i) for i in range(TOP)]
-        last_grouped = grouped_ring[(len(UNITS) - 1) % len(grouped_ring)]
-        cT = last_grouped[:].rearrange("t c k -> t (c k)").rearrange("t (b u p e) -> t b u p e", b=4, u=2, e=2)
         wp_raw = keep.tile([P, PACK, M], F32, name="wp_raw")
-        wp_bf = keep.tile([P, M, PACK], BF16, name="wp_bf", align_bytes=64)
-        wp_words = keep.tile([P, M], U32, name="wp_words", align_bytes=64)
-        wp_bytes = keep.tile([P, M], U8, name="wp_bytes", align_bytes=64)
         bias = {}
         sums = {}
-        raw_of = {}
+
+        def load_bias(e0, e1, pitch):
+            part = keep.tile([P, TILES, pitch], F32, name="bias%d" % e0)
+            nc.sync.dma_start(out=part[:, :, 0:e1 - e0], in_=b[:, e0:e1].rearrange("(j p) e -> p j e", p=P))
+            for e in range(e0, e1):
+                for j in range(TILES):
+                    bias[(e, j)] = part[:, j, e - e0:e - e0 + 1]
 
         def run_unit(u):
-            raw = take(raw_ring, "raw")
-            raw_of[u] = raw
-            col = 0
-            for e, j0, nj in UNITS[u]:
+            raw = raw_tiles[u % RAW_TILES]
+            width = 0
+            for e, j0, count in UNITS[u]:
                 nc.sync.dma_start(
-                    out=raw[:, :, col:col + nj * P],
-                    in_=w[e].rearrange("(p j) n -> p j n", j=PACK)[:, :, j0 * P:(j0 + nj) * P],
+                    out=raw[:, :, width:width + count * P],
+                    in_=w[e].rearrange("(p r) n -> p r n", r=PACK)[:, :, j0 * P:(j0 + count) * P],
                 )
-                col += nj * P
-            for at, e0, ne, j0, nj in BIAS_LOADS:
-                if at == u:
-                    part = keep.tile([P, nj, ne], F32, name="bias_%d_%d" % (e0, j0))
-                    with nc.allow_non_contiguous_dma(reason="a few bias columns"):
-                        nc.sync.dma_start(
-                            out=part[:], in_=b[j0 * P:(j0 + nj) * P, e0:e0 + ne].rearrange("(j p) e -> p j e", p=P)
-                        )
-                    for e in range(ne):
-                        for j in range(nj):
-                            bias[(e0 + e, j0 + j)] = part[:, j, e:e + 1]
-            if u == WP_AFTER:
-                nc.sync.dma_start(out=wp_raw[:], in_=wp.rearrange("(p j) f -> p j f", j=PACK))
-            grouped = take(grouped_ring, "grouped")
+                width += count * P
+            if u == 0:
+                load_bias(FIRST_EXPERTS, E, 16)
+            if u == FIRST_BIAS_UNIT:
+                load_bias(0, FIRST_EXPERTS, 8)
+            if u == LAST_UNIT:
+                nc.sync.dma_start(out=wp_raw[:], in_=wp.rearrange("(p r) f -> p r f", r=PACK))
+            rounded = rounded_tiles[u % ROUNDED_TILES]
             if VECTOR_COLS[u] > 0:
-                interleave(nc.vector.tensor_copy, grouped, raw, 0, VECTOR_COLS[u])
-            if VECTOR_COLS[u] < col:
-                interleave(nc.scalar.copy, grouped, raw, VECTOR_COLS[u], col)
-            words = take(words_ring, "words")
-            scales = take(scales_ring, "scales")
-            nc.vector.quantize_mx(
-                out=words[:, 0:col].bitcast(FP8X4), scales=scales[:, 0:col],
-                in_=grouped[:, 0:col, :].rearrange("p c t -> p (c t)"),
-            )
-            parts = [(e, j) for e, j0, nj in UNITS[u] for j in range(j0, j0 + nj)]
+                interleave(nc.vector.tensor_copy, rounded, raw, 0, VECTOR_COLS[u])
+            if VECTOR_COLS[u] < width:
+                interleave(nc.scalar.copy, rounded, raw, VECTOR_COLS[u], width)
+            words = word_tiles[u % QUANTISED_TILES]
+            scales = scale_tiles[u % QUANTISED_TILES]
+            quantise(nc, words[:, 0:width], scales[:, 0:width], rounded[:, 0:width, :])
+            bank = banks[(u + UNIT_BANKS) % 8] if u < WHOLE + PAIRS else banks[u % UNIT_BANKS]
+            parts = [(e, j) for e, j0, count in UNITS[u] for j in range(j0, j0 + count)]
             for q, (e, j) in enumerate(parts):
                 cols = slice(q * P, (q + 1) * P)
                 slots = slice(e * C, (e + 1) * C)
-                sums[(e, j)] = banks[BANK_OF[u]][:, cols]
-                nc.tensor.matmul_mx(
-                    out=sums[(e, j)],
-                    lhsT=words[:, cols].bitcast(FP8X4), lhsT_scale=scales[:, cols],
-                    rhs=slot_words[:, slots].bitcast(FP8X4), rhs_scale=slot_bytes[:, slots],
-                    start=True, stop=True,
-                )
+                sums[(e, j)] = bank[:, cols]
+                multiply(nc, sums[(e, j)], words[:, cols], scales[:, cols], slot_words[:, slots], slot_scales[:, slots])
 
-        def product(j, i, t0, nt, prod):
+        def add_product(j, i, t0, count, product):
             nc.vector.tensor_tensor(
-                prod[:, 0:nt],
-                y[j][:].indirect(pos_sb[i][:, t0 // 16:(t0 + nt) // 16]),
-                gate_sb[:, i, t0:t0 + nt],
+                product[:, 0:count],
+                y[j][:].indirect(pos_sb[i][:, t0 // 16:(t0 + count) // 16]),
+                gate_sb[:, i, t0:t0 + count],
                 MULT,
             )
-            for blk in range(nt // P):
+            for blk in range(count // P):
                 nc.tensor.matmul(
-                    banks[4 + t0 // P + blk][:, j * P:(j + 1) * P], prod[:, blk * P:(blk + 1) * P], ident[:],
+                    c_banks[t0 // P + blk][:, j * P:(j + 1) * P], product[:, blk * P:(blk + 1) * P], ident[:],
                     start=(i == 0), stop=(i == TOP - 1), is_transpose=True,
                 )
 
-        def round_sums(copy, blk, j0, nj):
-            copy(
-                cT[:, blk, :, 32 * j0:32 * (j0 + nj), :],
-                banks[4 + blk][:, j0 * P:(j0 + nj) * P].rearrange("t (p u e) -> t u p e", u=2, e=2),
+        for u in range(len(UNITS)):
+            run_unit(u)
+            for e, j in sums_read_after(u):
+                nc.scalar.activation(y[j][:, e * C:(e + 1) * C], sums[(e, j)], RELU, bias=bias[(e, j)])
+            if u == LISTS_UNIT:
+                for i, pos in enumerate((pos1, pos2, pos3, pos4)):
+                    nc.sync.dma_start(pos_sb[i][:], pos)
+            j, place = divmod(u - WHOLE - PAIRS, PAIRS)
+            if j >= 0:
+                for i in range(TOP):
+                    if min(i + 1, PAIRS - 1) == place:
+                        add_product(j, i, 0, T, raw_tiles[(u - place + i) % RAW_TILES][:, 0, :])
+
+        c_turned = (
+            rounded_tiles[LAST_UNIT % ROUNDED_TILES][:]
+            .rearrange("t c r -> t (c r)")
+            .rearrange("t (b h p e) -> t b h p e", b=BLOCKS, h=2, e=2)
+        )
+
+        def round_c(blk, j0, j1):
+            nc.scalar.copy(
+                c_turned[:, blk, :, 32 * j0:32 * j1, :],
+                c_banks[blk][:, j0 * P:j1 * P].rearrange("t (p h e) -> t h p e", h=2, e=2),
             )
 
-        rounded = {}
+        last_tile = TILES - 1
+        for blk in range(BLOCKS):
+            round_c(blk, 0, last_tile)
 
-        def turn_piece(j, t0, nt, how):
-            nblk = nt // P
-            c_bf = take(cbf_ring, "cbf")
-            rounded[t0] = c_bf
-            for blk in range(nblk):
-                tb = t0 // P + blk
-                round_sums(copies[how[0]], tb, j, 1)
-                turned = bank()
-                for u in range(2):
+        wp_rounded = keep.tile([P, M, PACK], BF16, name="wp_rounded", align_bytes=64)
+        wp_words = keep.tile([P, M], U32, name="wp_words", align_bytes=64)
+        wp_scales = keep.tile([P, M], U8, name="wp_scales", align_bytes=64)
+        for c0, c1 in WP_SCALAR_CUTS:
+            interleave(nc.scalar.copy, wp_rounded, wp_raw, c0, c1)
+        interleave(nc.vector.tensor_copy, wp_rounded, wp_raw, WP_SCALAR_CUTS[-1][1], M)
+        quantise(nc, wp_words[:], wp_scales[:], wp_rounded[:])
+
+        products = tiles("product", 2 * TOP, [P, HALF], F32)
+        c_rounded = tiles("c_rounded", 2, [P, HALF, PACK], BF16)
+        c_words = tiles("c_words", 2, [P, HALF], U32)
+        c_scales = tiles("c_scales", 2, [P, HALF], U8)
+        staged = tiles("staged", 4, [P, 2, HALF], F32)
+        move_pairs = (nc.vector.tensor_copy, nc.scalar.copy)
+        move_result = (nc.scalar.copy, nc.scalar.copy, nc.scalar.copy, nc.vector.tensor_copy)
+
+        for half in range(2):
+            for i in range(TOP):
+                add_product(last_tile, i, half * HALF, HALF, products[half * TOP + i])
+            for q in range(2):
+                blk = 2 * half + q
+                round_c(blk, last_tile, TILES)
+                for h in range(2):
                     nc.tensor.transpose(
-                        turned[:, u * P:(u + 1) * P],
-                        cT[:, tb, u, :, :].rearrange("t p e -> t (p e)").bitcast(F32),
+                        banks[blk][:, h * P:(h + 1) * P],
+                        c_turned[:, blk, h, :, :].rearrange("t p e -> t (p e)").bitcast(F32),
                         ident[:],
                     )
-                copies[how[1]](
-                    c_bf[:, blk * P:(blk + 1) * P, :].rearrange("p t k -> p (t k)").bitcast(F32).rearrange("p (t u) -> p t u", u=2),
-                    turned[:, 0:2 * P].rearrange("p (u t) -> p t u", u=2),
+                move_pairs[half](
+                    c_rounded[half][:, q * P:(q + 1) * P, :]
+                    .rearrange("p t r -> p (t r)")
+                    .bitcast(F32)
+                    .rearrange("p (t h) -> p t h", h=2),
+                    banks[blk][:, 0:2 * P].rearrange("p (h t) -> p t h", h=2),
                 )
 
-        def project(t0, nt, how):
-            c_bf = rounded[t0]
-            c_words = take(cw_ring, "cw")
-            c_bytes = take(cb_ring, "cb")
-            nc.vector.quantize_mx(
-                out=c_words[:, 0:nt].bitcast(FP8X4), scales=c_bytes[:, 0:nt],
-                in_=c_bf[:, 0:nt, :].rearrange("p t k -> p (t k)"),
-            )
-            for half in range(2):
-                res = bank()
+        for half in range(2):
+            quantise(nc, c_words[half][:], c_scales[half][:], c_rounded[half][:])
+            for rows in range(2):
+                r = 2 * half + rows
                 for q in range(2):
-                    f = slice((2 * half + q) * P, (2 * half + q + 1) * P)
-                    nc.tensor.matmul_mx(
-                        out=res[:, q * nt:(q + 1) * nt],
-                        lhsT=wp_words[:, f].bitcast(FP8X4), lhsT_scale=wp_bytes[:, f],
-                        rhs=c_words[:, 0:nt].bitcast(FP8X4), rhs_scale=c_bytes[:, 0:nt],
-                        start=True, stop=True,
+                    f = slice((2 * rows + q) * P, (2 * rows + q + 1) * P)
+                    multiply(
+                        nc, banks[r][:, q * HALF:(q + 1) * HALF],
+                        wp_words[:, f], wp_scales[:, f], c_words[half][:], c_scales[half][:],
                     )
-                staged = take(staged_ring, "staged")
-                copies[how[2 + half]](staged[:, 0:2 * nt], res[:, 0:2 * nt])
+                move_result[r](staged[r][:].rearrange("p q t -> p (q t)"), banks[r][:])
                 nc.sync.dma_start(
-                    out=out[half * 256:(half + 1) * 256, t0:t0 + nt].rearrange("(q p) t -> p q t", p=P),
-                    in_=staged[:, 0:2 * nt].rearrange("p (q t) -> p q t", q=2),
+                    out=out[rows * 2 * P:(rows + 1) * 2 * P, half * HALF:(half + 1) * HALF].rearrange(
+                        "(q p) t -> p q t", p=P
+                    ),
+                    in_=staged[r][:],
                 )
-
-        used = {}
-        for u in range(len(UNITS) + COMBINE_LAG):
-            if u < len(UNITS):
-                run_unit(u)
-            for e, j in EMPTY_AFTER.get(u, []):
-                nc.scalar.activation(y[j][:, e * C:(e + 1) * C], sums[(e, j)], RELU, bias=bias[(e, j)])
-            for i in range(TOP):
-                if GATE_AT[i] == u:
-                    nc.sync.dma_start(pos_sb[i][:], (pos1, pos2, pos3, pos4)[i])
-            for q, (v, at) in enumerate(PROD_IN):
-                if at == u:
-                    used[v] = used.get(v, -1) + 1
-                    product(q // TOP, q % TOP, 0, T, raw_of[v][:, used[v], :] if v >= 0 else take(prod_ring, "prod"))
-            if u == WP_TEXT:
-                for c0, c1, eng in WP_CUTS:
-                    interleave(copies[eng], wp_bf, wp_raw, c0, c1)
-                nc.vector.quantize_mx(
-                    out=wp_words[:].bitcast(FP8X4), scales=wp_bytes[:], in_=wp_bf[:].rearrange("p c t -> p (c t)")
-                )
-        for blk in range(4):
-            round_sums(nc.scalar.copy, blk, 0, 3)
-        starts = [sum(PIECES[:r]) for r in range(len(PIECES))]
-        for what, r in TAIL_ORDER:
-            if what == "g":
-                for i in range(TOP):
-                    product(3, i, LAST_CUTS[r][0], LAST_CUTS[r][1], take(prod_ring, "prod"))
-            elif what == "t":
-                turn_piece(3, starts[r], PIECES[r], TAIL[r])
-            else:
-                project(starts[r], PIECES[r], TAIL[r])

from contextlib import ExitStack

import concourse.mybir as mybir
from concourse.masks import make_identity

K, T, E, C, N, M, TOP = 512, 512, 16, 128, 512, 512, 4
S = E * C
P = 128
PACK = 4
TILES = N // P
BLOCKS = T // P
FLOPS = 2 * K * N * S + 2 * N * M * T
BYTES = 4 * (K * T + E * K * N + N * E + N * M + TOP * T + M * T) + 2 * P * (S + TOP * T) // 16

F32 = mybir.dt.float32
BF16 = mybir.dt.bfloat16
U32 = mybir.dt.uint32
U16 = mybir.dt.uint16
U8 = mybir.dt.uint8
FP8X4 = mybir.dt.float8_e4m3fn_x4
RELU = mybir.ActivationFunctionType.Relu
MULT = mybir.AluOpType.mult

SPLIT = 8
WHOLE = E - SPLIT
PAIRS = SPLIT // 2
UNITS = [[(e, 0, TILES)] for e in range(WHOLE)] + [
    [(e, j, 1), (e + 1, j, 1)] for j in range(TILES) for e in range(WHOLE, E, 2)
]
LAST_UNIT = len(UNITS) - 1

VECTOR_COLS = (
    [0, 0, 512, 0, 0, 256, 512, 512]
    + [128, 128, 256, 256]
    + [256, 64, 0, 0]
    + [64, 0, 0, 0]
    + [64, 0, 0, 0]
)
WP_SCALAR_CUTS = [(0, 256), (256, 384)]
HALF = T // 2

FIRST_EXPERTS = 4
FIRST_BIAS_UNIT = 5
LISTS_UNIT = 3
TOKEN_GATHER = 384

RAW_TILES = 9
ROUNDED_TILES = 6
QUANTISED_TILES = 4
UNIT_BANKS = 4


def interleave(copy, rounded, raw, c0, c1):
    copy(
        rounded[:, c0:c1, :].rearrange("p (c i) r -> p c r i", i=2),
        raw[:, :, c0:c1].rearrange("p r (c i) -> p c r i", i=2),
    )


def quantise(nc, words, scales, rounded):
    nc.vector.quantize_mx(out=words.bitcast(FP8X4), scales=scales, in_=rounded.rearrange("p c r -> p (c r)"))


def multiply(nc, result, left_words, left_scales, right_words, right_scales):
    nc.tensor.matmul_mx(
        out=result,
        lhsT=left_words.bitcast(FP8X4), lhsT_scale=left_scales,
        rhs=right_words.bitcast(FP8X4), rhs_scale=right_scales,
        start=True, stop=True,
    )


def sums_read_after(u):
    if u == FIRST_BIAS_UNIT:
        return [(e, j) for j in range(TILES) for e in range(FIRST_EXPERTS)]
    if u == WHOLE - 1:
        return [(e, j) for j in range(TILES) for e in range(FIRST_EXPERTS, WHOLE)]
    if u >= WHOLE:
        return [(e, j) for e, j, tiles in UNITS[u]]
    return []


def tile_moe_nxt_lin_relu_kernel(
    tc, xT, w, b, wp, gate, offs, pos1, pos2, pos3, pos4, out
):
    nc = tc.nc
    with ExitStack() as ctx:
        keep = ctx.enter_context(tc.tile_pool(name="keep", bufs=1))
        psum = ctx.enter_context(tc.psum_pool(name="psum", bufs=1))
        banks = [psum.tile([P, 512], F32, name="bank%d" % r) for r in range(8)]
        c_banks = banks[UNIT_BANKS:]

        def tiles(name, count, shape, dtype):
            return [keep.tile(shape, dtype, name="%s%d" % (name, r), align_bytes=64) for r in range(count)]

        raw_tiles = tiles("raw", RAW_TILES, [P, PACK, N], F32)
        rounded_tiles = tiles("rounded", ROUNDED_TILES, [P, N, PACK], BF16)
        word_tiles = tiles("words", QUANTISED_TILES, [P, N], U32)
        scale_tiles = tiles("scales", QUANTISED_TILES, [P, N], U8)

        gate_rows = keep.tile([P, T], F32, name="gate_rows")
        nc.gpsimd.memset(gate_rows[:], 0.0)
        x_raw = keep.tile([P, PACK, T], F32, name="x_raw")
        nc.sync.dma_start(out=x_raw[:], in_=xT.rearrange("(p r) t -> p r t", r=PACK))
        offs_sb = keep.tile([P, S // 16], U16, name="offs_sb")
        nc.sync.dma_start(offs_sb[:], offs)
        x_words = keep.tile([P, T], U32, name="x_words", align_bytes=64)
        x_scales = keep.tile([P, T], U8, name="x_scales", align_bytes=64)
        nc.gpsimd.memset(x_scales[:], 0)
        ident = keep.tile([P, P], F32, name="ident")
        make_identity(nc, ident[:])
        nc.sync.dma_start(out=gate_rows[0:TOP, :], in_=gate[:, 0, :])
        x_rounded = keep.tile([P, T, PACK], BF16, name="x_rounded", align_bytes=64)
        interleave(nc.vector.tensor_copy, x_rounded, x_raw, 0, HALF)
        interleave(nc.scalar.copy, x_rounded, x_raw, HALF, T)
        for t0 in (0, HALF):
            tokens = slice(t0, t0 + HALF)
            quantise(nc, x_words[:, tokens], x_scales[:, tokens], x_rounded[:, tokens, :])
        slot_words = keep.tile([P, S], U32, name="slot_words", align_bytes=64)
        slot_scales = keep.tile([P, S], U8, name="slot_scales", align_bytes=64)
        for s0 in range(0, S, TOKEN_GATHER):
            s1 = min(S, s0 + TOKEN_GATHER)
            entries = offs_sb[:, s0 // 16:s1 // 16]
            nc.vector.tensor_copy(slot_words[:, s0:s1], x_words[:].indirect(entries))
            nc.vector.tensor_copy(slot_scales[:, s0:s1], x_scales[:].indirect(entries))

        for blk in range(BLOCKS):
            nc.tensor.transpose(c_banks[0][:, blk * P:(blk + 1) * P], gate_rows[:, blk * P:(blk + 1) * P], ident[:])
        gate_cols = keep.tile([P, BLOCKS, TOP], F32, name="gate_cols")
        nc.scalar.copy(gate_cols[:], c_banks[0][:].rearrange("t (b r) -> t b r", b=BLOCKS)[:, :, 0:TOP])
        gate_sb = keep.tile([P, TOP, T], F32, name="gate_sb")
        for i in range(TOP):
            for blk in range(BLOCKS):
                nc.tensor.transpose(
                    banks[i][:, blk * P:(blk + 1) * P], gate_cols[:, blk, i:i + 1].to_broadcast([P, P]), ident[:]
                )
            nc.scalar.copy(gate_sb[:, i, :], banks[i][:])

        y = [keep.tile([P, S], F32, name="y%d" % j) for j in range(TILES)]
        pos_sb = [keep.tile([P, T // 16], U16, name="pos%d" % i) for i in range(TOP)]
        wp_raw = keep.tile([P, PACK, M], F32, name="wp_raw")
        bias = {}
        sums = {}

        def load_bias(e0, e1, pitch):
            part = keep.tile([P, TILES, pitch], F32, name="bias%d" % e0)
            nc.sync.dma_start(out=part[:, :, 0:e1 - e0], in_=b[:, e0:e1].rearrange("(j p) e -> p j e", p=P))
            for e in range(e0, e1):
                for j in range(TILES):
                    bias[(e, j)] = part[:, j, e - e0:e - e0 + 1]

        def run_unit(u):
            raw = raw_tiles[u % RAW_TILES]
            width = 0
            for e, j0, count in UNITS[u]:
                nc.sync.dma_start(
                    out=raw[:, :, width:width + count * P],
                    in_=w[e].rearrange("(p r) n -> p r n", r=PACK)[:, :, j0 * P:(j0 + count) * P],
                )
                width += count * P
            if u == 0:
                load_bias(FIRST_EXPERTS, E, 16)
            if u == FIRST_BIAS_UNIT:
                load_bias(0, FIRST_EXPERTS, 8)
            if u == LAST_UNIT:
                nc.sync.dma_start(out=wp_raw[:], in_=wp.rearrange("(p r) f -> p r f", r=PACK))
            rounded = rounded_tiles[u % ROUNDED_TILES]
            if VECTOR_COLS[u] > 0:
                interleave(nc.vector.tensor_copy, rounded, raw, 0, VECTOR_COLS[u])
            if VECTOR_COLS[u] < width:
                interleave(nc.scalar.copy, rounded, raw, VECTOR_COLS[u], width)
            words = word_tiles[u % QUANTISED_TILES]
            scales = scale_tiles[u % QUANTISED_TILES]
            quantise(nc, words[:, 0:width], scales[:, 0:width], rounded[:, 0:width, :])
            bank = banks[(u + UNIT_BANKS) % 8] if u < WHOLE + PAIRS else banks[u % UNIT_BANKS]
            parts = [(e, j) for e, j0, count in UNITS[u] for j in range(j0, j0 + count)]
            for q, (e, j) in enumerate(parts):
                cols = slice(q * P, (q + 1) * P)
                slots = slice(e * C, (e + 1) * C)
                sums[(e, j)] = bank[:, cols]
                multiply(nc, sums[(e, j)], words[:, cols], scales[:, cols], slot_words[:, slots], slot_scales[:, slots])

        def add_product(j, i, t0, count, product):
            nc.vector.tensor_tensor(
                product[:, 0:count],
                y[j][:].indirect(pos_sb[i][:, t0 // 16:(t0 + count) // 16]),
                gate_sb[:, i, t0:t0 + count],
                MULT,
            )
            for blk in range(count // P):
                nc.tensor.matmul(
                    c_banks[t0 // P + blk][:, j * P:(j + 1) * P], product[:, blk * P:(blk + 1) * P], ident[:],
                    start=(i == 0), stop=(i == TOP - 1), is_transpose=True,
                )

        for u in range(len(UNITS)):
            run_unit(u)
            for e, j in sums_read_after(u):
                nc.scalar.activation(y[j][:, e * C:(e + 1) * C], sums[(e, j)], RELU, bias=bias[(e, j)])
            if u == LISTS_UNIT:
                for i, pos in enumerate((pos1, pos2, pos3, pos4)):
                    nc.sync.dma_start(pos_sb[i][:], pos)
            j, place = divmod(u - WHOLE - PAIRS, PAIRS)
            if j >= 0:
                for i in range(TOP):
                    if min(i + 1, PAIRS - 1) == place:
                        add_product(j, i, 0, T, raw_tiles[(u - place + i) % RAW_TILES][:, 0, :])

        c_turned = (
            rounded_tiles[LAST_UNIT % ROUNDED_TILES][:]
            .rearrange("t c r -> t (c r)")
            .rearrange("t (b h p e) -> t b h p e", b=BLOCKS, h=2, e=2)
        )

        def round_c(blk, j0, j1):
            nc.scalar.copy(
                c_turned[:, blk, :, 32 * j0:32 * j1, :],
                c_banks[blk][:, j0 * P:j1 * P].rearrange("t (p h e) -> t h p e", h=2, e=2),
            )

        last_tile = TILES - 1
        for blk in range(BLOCKS):
            round_c(blk, 0, last_tile)

        wp_rounded = keep.tile([P, M, PACK], BF16, name="wp_rounded", align_bytes=64)
        wp_words = keep.tile([P, M], U32, name="wp_words", align_bytes=64)
        wp_scales = keep.tile([P, M], U8, name="wp_scales", align_bytes=64)
        for c0, c1 in WP_SCALAR_CUTS:
            interleave(nc.scalar.copy, wp_rounded, wp_raw, c0, c1)
        interleave(nc.vector.tensor_copy, wp_rounded, wp_raw, WP_SCALAR_CUTS[-1][1], M)
        quantise(nc, wp_words[:], wp_scales[:], wp_rounded[:])

        products = tiles("product", 2 * TOP, [P, HALF], F32)
        c_rounded = tiles("c_rounded", 2, [P, HALF, PACK], BF16)
        c_words = tiles("c_words", 2, [P, HALF], U32)
        c_scales = tiles("c_scales", 2, [P, HALF], U8)
        staged = tiles("staged", 4, [P, 2, HALF], F32)
        move_pairs = (nc.vector.tensor_copy, nc.scalar.copy)
        move_result = (nc.scalar.copy, nc.scalar.copy, nc.scalar.copy, nc.vector.tensor_copy)

        for half in range(2):
            for i in range(TOP):
                add_product(last_tile, i, half * HALF, HALF, products[half * TOP + i])
            for q in range(2):
                blk = 2 * half + q
                round_c(blk, last_tile, TILES)
                for h in range(2):
                    nc.tensor.transpose(
                        banks[blk][:, h * P:(h + 1) * P],
                        c_turned[:, blk, h, :, :].rearrange("t p e -> t (p e)").bitcast(F32),
                        ident[:],
                    )
                move_pairs[half](
                    c_rounded[half][:, q * P:(q + 1) * P, :]
                    .rearrange("p t r -> p (t r)")
                    .bitcast(F32)
                    .rearrange("p (t h) -> p t h", h=2),
                    banks[blk][:, 0:2 * P].rearrange("p (h t) -> p t h", h=2),
                )

        for half in range(2):
            quantise(nc, c_words[half][:], c_scales[half][:], c_rounded[half][:])
            for rows in range(2):
                r = 2 * half + rows
                for q in range(2):
                    f = slice((2 * rows + q) * P, (2 * rows + q + 1) * P)
                    multiply(
                        nc, banks[r][:, q * HALF:(q + 1) * HALF],
                        wp_words[:, f], wp_scales[:, f], c_words[half][:], c_scales[half][:],
                    )
                move_result[r](staged[r][:].rearrange("p q t -> p (q t)"), banks[r][:])
                nc.sync.dma_start(
                    out=out[rows * 2 * P:(rows + 1) * 2 * P, half * HALF:(half + 1) * HALF].rearrange(
                        "(q p) t -> p q t", p=P
                    ),
                    in_=staged[r][:],
                )
